import numpy as np
import ml_dtypes


def mxq(x, axis, fmt="e4m3"):
    dtype, down = {"e4m3": (ml_dtypes.float8_e4m3fn, 7), "e5m2": (ml_dtypes.float8_e5m2, 14)}[fmt]
    v = np.moveaxis(np.asarray(x, np.float32).astype(ml_dtypes.bfloat16).astype(np.float64), axis, -1)
    blocks = v.reshape(v.shape[:-1] + (-1, 32))
    amax = np.abs(blocks).max(-1, keepdims=True)
    byte = np.maximum(np.where(amax > 0, np.frexp(amax)[1] - 1 + 127, 0) - down, 1)
    scale = np.exp2(byte - 127.0)
    codes = (blocks / scale).astype(np.float32).astype(dtype).astype(np.float64)
    return np.moveaxis((codes * scale).reshape(v.shape), -1, axis)


WIDE = False


def mx_kscale(k):
    if not WIDE:
        return np.ones(k)
    levels = np.array([10, -10, 5, -5, 0])
    if k % 512:
        return np.exp2(np.random.permutation(np.resize(levels, k // 32))).repeat(32)
    a = np.empty((k // 512, 16))
    for p in range(k // 512):
        a[p, :8] = np.random.permutation(np.resize(levels, 8))
        for g in range(8):
            far = levels[np.abs(levels - a[p, g]) >= 10]
            a[p, g + 8] = far[np.random.randint(len(far))]
    return np.exp2(a.ravel()).repeat(32)


def f64(x):
    return np.asarray(x).astype(np.float64)


E2M1 = np.array([0.0, 0.5, 1.0, 1.5, 2.0, 3.0, 4.0, 6.0, -0.0, -0.5, -1.0, -1.5, -2.0, -3.0, -4.0, -6.0])


def pack_weight(w, fmt):
    k, n = w.shape
    w = f64(np.asarray(w, np.float32).astype(ml_dtypes.bfloat16)).reshape(k // 32, 32, n)
    amax = np.abs(w).max(1)
    if fmt == "e4m3":
        byte = np.frexp(amax)[1] - 1 + 127 - 7
    else:
        mant, ex = np.frexp(amax / 6.0)
        byte = np.where(mant > 0.5, ex, ex - 1) + 127
    byte = np.clip(np.where(amax > 0, byte, 1), 1, 254)
    scaled = (w * np.exp2(127.0 - byte)[:, None, :]).reshape(k, n).astype(np.float32)
    by_word = np.ascontiguousarray(scaled.reshape(k // 512, 128, 4, n).transpose(0, 1, 3, 2))
    if fmt == "e4m3":
        words = by_word.astype(ml_dtypes.float8_e4m3fn).view(np.uint8)
    else:
        c = by_word.astype(ml_dtypes.float4_e2m1fn).view(np.uint8) & 0xF
        words = (c[..., 0::2] | (c[..., 1::2] << 4)).reshape(k // 512, 128, 2 * n)
    return np.ascontiguousarray(words), np.ascontiguousarray(byte.astype(np.uint8).reshape(k // 512, 16, n))


def unpack_weight(words, scales, fmt):
    g, _, n = scales.shape
    words = np.ascontiguousarray(words).reshape(g, 128, n, -1)
    if fmt == "e4m3":
        vals = words.view(ml_dtypes.float8_e4m3fn).astype(np.float64)
    else:
        nib = np.empty((g, 128, n, 4), np.uint8)
        nib[..., 0::2] = words & 0xF
        nib[..., 1::2] = words >> 4
        vals = E2M1[nib]
    vals = vals * np.repeat(np.exp2(scales.astype(np.float64) - 127.0), 8, axis=1)[..., None]
    return vals.transpose(0, 1, 3, 2).reshape(g * 512, n)


def bf(x):
    return np.asarray(x, np.float32).astype(ml_dtypes.bfloat16)


def planes(Y):
    r, m = Y.shape
    b = f64(bf(Y)).reshape(r // 32, 32, m)
    amax = np.abs(b).max(1)
    byte = np.clip(np.where(amax > 0, np.frexp(amax)[1] - 1 + 127 - 7, 1), 1, 254)
    codes = (b * np.exp2(127.0 - byte)[:, None, :]).reshape(r, m).astype(np.float32).astype(ml_dtypes.float8_e4m3fn).view(np.uint8)
    words = codes.reshape(r // 512, 128, 4, m).transpose(0, 1, 3, 2)
    return np.ascontiguousarray(words), np.ascontiguousarray(byte.astype(np.uint8).reshape(r // 512, 16, m))


K, L, Q, I, N = 512, 512, 512, 512, 512


def setup_inputs():
    n = np.random.standard_normal
    fk = mx_kscale(K)
    fl = mx_kscale(L)
    fi = mx_kscale(I)
    qap = pack_weight(n((K, Q)) * 0.06 * fk[:, None], "e2m1")
    kap = pack_weight(n((K, I)) / fk[:, None], "e4m3")
    qbp = pack_weight(n((L, Q)) * 0.06 * fl[:, None], "e2m1")
    kbp = pack_weight(n((L, I)) / fl[:, None], "e4m3")
    vop = pack_weight(n((I, N)) * 1 / np.sqrt(I) / fi[:, None], "e2m1")
    wyp = pack_weight(n((K, N)) * 10.0 / np.sqrt(K) / fk[:, None], "e4m3")
    return {
        "qa_words": qap[0],
        "qa_scales": qap[1],
        "ka_words": kap[0],
        "ka_scales": kap[1],
        "qb_words": qbp[0],
        "qb_scales": qbp[1],
        "kb_words": kbp[0],
        "kb_scales": kbp[1],
        "fi": (np.random.uniform(0.5, 2.0, (I, 1)) * fi[:, None]).astype(np.float32),
        "vo_words": vop[0],
        "vo_scales": vop[1],
        "wy_words": wyp[0],
        "wy_scales": wyp[1],
    }


def reference(qa_words, qa_scales, ka_words, ka_scales, qb_words, qb_scales, kb_words, kb_scales, fi, vo_words, vo_scales, wy_words, wy_scales):
    qau = unpack_weight(qa_words, qa_scales, "e2m1")
    kau = unpack_weight(ka_words, ka_scales, "e4m3")
    qbu = unpack_weight(qb_words, qb_scales, "e2m1")
    kbu = unpack_weight(kb_words, kb_scales, "e4m3")
    vou = unpack_weight(vo_words, vo_scales, "e2m1")
    wyu = unpack_weight(wy_words, wy_scales, "e4m3")
    a = qau.T @ kau + qbu.T @ kbu
    p = np.maximum(a, 0.0)
    pt = p.T
    pw = pt * f64(fi)
    pwq = mxq(pw, 0, "e4m3")
    y = vou.T @ pwq + wyu.T @ qau
    words, scales = planes(y)
    return y, words, scales

@@ -1,0 +1,204 @@
+from contextlib import ExitStack
+
+import concourse.mybir as mybir
+
+F32 = mybir.dt.float32
+BF16 = mybir.dt.bfloat16
+I32 = mybir.dt.int32
+U32 = mybir.dt.uint32
+U16 = mybir.dt.uint16
+U8 = mybir.dt.uint8
+FP8X4 = mybir.dt.float8_e4m3fn_x4
+FP4X4 = mybir.dt.float4_e2m1fn_x4
+ALU = mybir.AluOpType
+
+P = 128
+PACK = 4
+W = 512
+CH = 128
+NCH = W // CH
+FLOPS = 4 * 2 * 512 * 512 * 512
+
+
+def tile_mix_positive_scores_carry_rows_pl_kernel(
+    tc, qa_words, qa_scales, ka_words, ka_scales, qb_words, qb_scales, kb_words, kb_scales,
+    fi, vo_words, vo_scales, wy_words, wy_scales, out_0, out_1, out_2,
+):
+    nc = tc.nc
+    with ExitStack() as ctx:
+        sb = ctx.enter_context(tc.tile_pool(name="sb", bufs=1))
+        ps = ctx.enter_context(tc.psum_pool(name="ps", bufs=1))
+        ctx.enter_context(tc.manual_schedule())
+
+        def tile(name, shape, dtype):
+            return sb.tile(shape, dtype, name=name, align_bytes=64)
+
+        ka_raw = tile("ka_raw", [P, W], U32)
+        kb_raw = tile("kb_raw", [P, W], U32)
+        wy_raw = tile("wy_raw", [P, W], U32)
+        vo_raw = tile("vo_raw", [P, 2 * W], U8)
+        qa_w = tile("qa_w", [P, 2 * W], U8)
+        qb_w = tile("qb_w", [P, 2 * W], U8)
+        ka_w = tile("ka_w", [P, W], U32)
+        kb_w = tile("kb_w", [P, W], U32)
+        wy_w = tile("wy_w", [P, W], U32)
+        vo_w = tile("vo_w", [P, 2 * W], U8)
+        ka_s = tile("ka_s", [P, W], U8)
+        kb_s = tile("kb_s", [P, W], U8)
+        wy_s = tile("wy_s", [P, W], U8)
+        vo_s = tile("vo_s", [P, W], U8)
+        rows1 = tile("rows1", [16, 6 * W], U8)
+        planes1 = tile("planes1", [P, 6 * W], U8)
+        fi_t = tile("fi_t", [P, PACK], F32)
+        y_codes = tile("y_codes", [P, W], U32)
+        y_scales = tile("y_scales", [P, W], U8)
+
+        def words8(ap):
+            return ap[0].rearrange("p c t -> p (c t)").bitcast(I32)
+
+        nc.vector.memset(planes1[:].bitcast(U32), 0)
+        nc.gpsimd.dma_start(out=fi_t[:], in_=fi.rearrange("(p t) o -> p (t o)", t=PACK))
+
+        queues = (nc.sync, nc.scalar)
+        for j, src in enumerate((ka_scales, qa_scales, kb_scales, qb_scales, wy_scales, vo_scales)):
+            queues[j // 4].dma_start(out=rows1[:, j * W:(j + 1) * W].bitcast(I32), in_=src[0].bitcast(I32))
+        nc.scalar.dma_start(out=ka_raw[:].bitcast(I32), in_=words8(ka_words))
+        nc.scalar.dma_start(out=qa_w[:].bitcast(I32), in_=qa_words[0].bitcast(I32))
+        for q in (0, 2, 1, 3):
+            nc.sync.dma_start(
+                out=planes1[32 * q:32 * q + 4, :].bitcast(I32), in_=rows1[4 * q:4 * q + 4, :].bitcast(I32)
+            )
+        nc.scalar.dma_start(out=kb_raw[:].bitcast(I32), in_=words8(kb_words))
+        nc.scalar.dma_start(out=qb_w[:].bitcast(I32), in_=qb_words[0].bitcast(I32))
+        nc.sync.dma_start(out=wy_raw[:].bitcast(I32), in_=words8(wy_words))
+        nc.sync.dma_start(out=vo_raw[:].bitcast(I32), in_=vo_words[0].bitcast(I32))
+
+        def deal_words32(engine_copy, dst, src):
+            engine_copy(
+                out=dst.rearrange("p (t b i) -> p b t i", t=PACK, i=4),
+                in_=src.rearrange("p (b i t) -> p b t i", t=PACK, i=4),
+            )
+
+        def deal_small(engine_copy, dst, src):
+            engine_copy(
+                out=dst.rearrange("p (t m) -> p t m", t=PACK),
+                in_=src.rearrange("p (m t) -> p t m", t=PACK),
+            )
+
+        deal_words32(nc.vector.tensor_copy, ka_w[:], ka_raw[:])
+        deal_words32(nc.scalar.copy, kb_w[:], kb_raw[:])
+        deal_small(nc.vector.tensor_copy, ka_s[:], planes1[:, 0:W])
+        deal_small(nc.vector.tensor_copy, kb_s[:], planes1[:, 2 * W:3 * W])
+        deal_words32(nc.scalar.copy, wy_w[:], wy_raw[:])
+        deal_small(nc.scalar.copy, vo_w[:].bitcast(U16), vo_raw[:].bitcast(U16))
+        deal_small(nc.vector.tensor_copy, wy_s[:], planes1[:, 4 * W:5 * W])
+        deal_small(nc.vector.tensor_copy, vo_s[:], planes1[:, 5 * W:6 * W])
+        qa_s = planes1[:, W:2 * W]
+        qb_s = planes1[:, 3 * W:4 * W]
+
+        a_bank = [ps.tile([P, PACK, CH], F32, name="a%d" % c) for c in range(NCH)]
+        y_bank = [ps.tile([P, PACK, CH], F32, name="y%d" % c) for c in range(NCH)]
+        pw_bf = [tile("pw_bf%d" % c, [P, CH * PACK], BF16) for c in range(NCH)]
+        pw_w = [tile("pw_w%d" % c, [P, CH], U32) for c in range(NCH)]
+        pw_s = [tile("pw_s%d" % c, [P, CH], U8) for c in range(NCH)]
+        y_f = [tile("y_f%d" % c, [P, PACK, CH], F32) for c in range(NCH)]
+        y_bf = [tile("y_bf%d" % c, [P, CH * PACK], BF16) for c in range(NCH)]
+        out_rows = out_0.rearrange("(p r) q -> p r q", r=PACK)
+        out_words = words8(out_1)
+
+        def cols(j, width=1):
+            return slice(j * CH * width, (j + 1) * CH * width)
+
+        def fp8_by_fp4(bank, c, w8, s8, w4, s4, first, last):
+            for t in range(PACK):
+                nc.tensor.matmul_mx(
+                    out=bank[:, t, :],
+                    lhsT=w8[:, cols(t)].bitcast(FP8X4), lhsT_scale=s8[:, cols(t)],
+                    rhs=w4[:, cols(c, 2)].bitcast(FP4X4), rhs_scale=s4[:, cols(c)],
+                    start=(first and t == 0), stop=(last and t == PACK - 1),
+                )
+
+        def scores(c):
+            fp8_by_fp4(a_bank[c], c, ka_w, ka_s, qa_w, qa_s, True, False)
+            fp8_by_fp4(a_bank[c], c, kb_w, kb_s, qb_w, qb_s, False, True)
+
+        def skip(c):
+            fp8_by_fp4(y_bank[c], c, wy_w, wy_s, qa_w, qa_s, True, False)
+
+        def carry(c):
+            for r in range(PACK):
+                nc.tensor.matmul_mx(
+                    out=y_bank[c][:, r, :],
+                    lhsT=vo_w[:, cols(r, 2)].bitcast(FP4X4), lhsT_scale=vo_s[:, cols(r)],
+                    rhs=pw_w[c][:].bitcast(FP8X4), rhs_scale=pw_s[c][:],
+                    start=False, stop=(r == PACK - 1),
+                )
+
+        def weigh(c):
+            nc.vector.scalar_tensor_tensor(
+                out=pw_bf[c][:].rearrange("p (q t) -> p q t", t=PACK),
+                in0=a_bank[c][:].rearrange("p t q -> p q t"),
+                scalar=0.0,
+                in1=fi_t[:].unsqueeze(1).to_broadcast([P, CH, PACK]),
+                op0=ALU.max, op1=ALU.mult,
+            )
+
+        def quantise_pw(c):
+            nc.vector.quantize_mx(out=pw_w[c][:].bitcast(FP8X4), scales=pw_s[c][:], in_=pw_bf[c][:])
+
+        def y_out(c):
+            nc.scalar.copy(out=y_f[c][:], in_=y_bank[c][:])
+            nc.sync.dma_start(out=out_rows[:, :, cols(c)], in_=y_f[c][:])
+
+        def y_round_scalar(c):
+            nc.scalar.copy(
+                out=y_bf[c][:].rearrange("p (q r) -> p q r", r=PACK),
+                in_=y_bank[c][:].rearrange("p r q -> p q r"),
+            )
+
+        def y_round_vector(c):
+            nc.vector.tensor_copy(
+                out=y_bf[c][:].rearrange("p (b i r) -> p b r i", r=PACK, i=4),
+                in_=y_f[c][:].rearrange("p r (b i) -> p b r i", i=4),
+            )
+
+        def quantise_y(c):
+            nc.vector.quantize_mx(out=y_codes[:, cols(c)].bitcast(FP8X4), scales=y_scales[:, cols(c)], in_=y_bf[c][:])
+            nc.sync.dma_start(out=out_words[:, cols(c)], in_=y_codes[:, cols(c)].bitcast(I32))
+
+        scores(0)
+        weigh(0)
+        quantise_pw(0)
+        scores(1)
+        weigh(1)
+        quantise_pw(1)
+        skip(0)
+        carry(0)
+        y_out(0)
+        y_round_scalar(0)
+        scores(2)
+        weigh(2)
+        quantise_pw(2)
+        skip(1)
+        carry(1)
+        y_out(1)
+        y_round_scalar(1)
+        quantise_y(0)
+        scores(3)
+        weigh(3)
+        quantise_pw(3)
+        skip(2)
+        carry(2)
+        y_out(2)
+        quantise_y(1)
+        skip(3)
+        carry(3)
+        y_round_vector(2)
+        y_out(3)
+        quantise_y(2)
+        y_round_vector(3)
+        quantise_y(3)
+        for q in range(4):
+            queues[q % 2].dma_start(
+                out=out_2[0, 4 * q:4 * q + 4, :].bitcast(I32), in_=y_scales[32 * q:32 * q + 4, :].bitcast(I32)
+            )

@@ -13,11 +13,14 @@ FP4X4 = mybir.dt.float4_e2m1fn_x4
 ALU = mybir.AluOpType
 
 P = 128
-PACK = 4
+SLOTS = 4
 W = 512
 CH = 128
-NCH = W // CH
-FLOPS = 4 * 2 * 512 * 512 * 512
+CHUNKS = W // CH
+BLOCKS = 16
+QUADS = 4
+RUN = 4
+FLOPS = 4 * 2 * W * W * W
 
 
 def tile_mix_positive_scores_carry_rows_pl_kernel(
@@ -25,6 +28,7 @@ def tile_mix_positive_scores_carry_rows_pl_kernel(
     fi, vo_words, vo_scales, wy_words, wy_scales, out_0, out_1, out_2,
 ):
     nc = tc.nc
+    queues = (nc.sync, nc.scalar)
     with ExitStack() as ctx:
         sb = ctx.enter_context(tc.tile_pool(name="sb", bufs=1))
         ps = ctx.enter_context(tc.psum_pool(name="ps", bufs=1))
@@ -32,6 +36,9 @@ def tile_mix_positive_scores_carry_rows_pl_kernel(
 
         def tile(name, shape, dtype):
             return sb.tile(shape, dtype, name=name, align_bytes=64)
+
+        def cols(j, width):
+            return slice(j * width, (j + 1) * width)
 
         ka_raw = tile("ka_raw", [P, W], U32)
         kb_raw = tile("kb_raw", [P, W], U32)
@@ -47,158 +54,179 @@ def tile_mix_positive_scores_carry_rows_pl_kernel(
         kb_s = tile("kb_s", [P, W], U8)
         wy_s = tile("wy_s", [P, W], U8)
         vo_s = tile("vo_s", [P, W], U8)
-        rows1 = tile("rows1", [16, 6 * W], U8)
-        planes1 = tile("planes1", [P, 6 * W], U8)
-        fi_t = tile("fi_t", [P, PACK], F32)
+        score_scales = (ka_scales, qa_scales, kb_scales, qb_scales)
+        out_scales = (wy_scales, vo_scales)
+        score_rows = tile("score_rows", [BLOCKS, len(score_scales) * W], U8)
+        score_planes = tile("score_planes", [P, len(score_scales) * W], U8)
+        out_rows = tile("out_rows", [BLOCKS, len(out_scales) * W], U8)
+        out_planes = tile("out_planes", [P, len(out_scales) * W], U8)
+        ka_plane, qa_s, kb_plane, qb_s = [score_planes[:, cols(j, W)] for j in range(len(score_scales))]
+        wy_plane, vo_plane = [out_planes[:, cols(j, W)] for j in range(len(out_scales))]
+        fi_t = tile("fi_t", [P, SLOTS], F32)
         y_codes = tile("y_codes", [P, W], U32)
         y_scales = tile("y_scales", [P, W], U8)
 
-        def words8(ap):
+        a_bank = [ps.tile([P, SLOTS, CH], F32, name="a%d" % c) for c in range(CHUNKS)]
+        y_bank = [ps.tile([P, SLOTS, CH], F32, name="y%d" % c) for c in range(CHUNKS)]
+        pw_bf = [tile("pw_bf%d" % c, [P, CH * SLOTS], BF16) for c in range(CHUNKS)]
+        pw_w = [tile("pw_w%d" % c, [P, CH], U32) for c in range(CHUNKS)]
+        pw_s = [tile("pw_s%d" % c, [P, CH], U8) for c in range(CHUNKS)]
+        y_f = [tile("y_f%d" % c, [P, SLOTS, CH], F32) for c in range(CHUNKS)]
+        y_bf = [tile("y_bf%d" % c, [P, CH * SLOTS], BF16) for c in range(CHUNKS)]
+
+        def as_words(ap):
             return ap[0].rearrange("p c t -> p (c t)").bitcast(I32)
 
-        nc.vector.memset(planes1[:].bitcast(U32), 0)
-        nc.gpsimd.dma_start(out=fi_t[:], in_=fi.rearrange("(p t) o -> p (t o)", t=PACK))
+        def load_rows(rows, sources):
+            for j, src in enumerate(sources):
+                queues[j % 2].dma_start(out=rows[0:BLOCKS, cols(j, W)].bitcast(I32), in_=src[0].bitcast(I32))
 
-        queues = (nc.sync, nc.scalar)
-        for j, src in enumerate((ka_scales, qa_scales, kb_scales, qb_scales, wy_scales, vo_scales)):
-            queues[j // 4].dma_start(out=rows1[:, j * W:(j + 1) * W].bitcast(I32), in_=src[0].bitcast(I32))
-        nc.scalar.dma_start(out=ka_raw[:].bitcast(I32), in_=words8(ka_words))
-        nc.scalar.dma_start(out=qa_w[:].bitcast(I32), in_=qa_words[0].bitcast(I32))
-        for q in (0, 2, 1, 3):
-            nc.sync.dma_start(
-                out=planes1[32 * q:32 * q + 4, :].bitcast(I32), in_=rows1[4 * q:4 * q + 4, :].bitcast(I32)
-            )
-        nc.scalar.dma_start(out=kb_raw[:].bitcast(I32), in_=words8(kb_words))
-        nc.scalar.dma_start(out=qb_w[:].bitcast(I32), in_=qb_words[0].bitcast(I32))
-        nc.sync.dma_start(out=wy_raw[:].bitcast(I32), in_=words8(wy_words))
-        nc.sync.dma_start(out=vo_raw[:].bitcast(I32), in_=vo_words[0].bitcast(I32))
-
-        def deal_words32(engine_copy, dst, src):
-            engine_copy(
-                out=dst.rearrange("p (t b i) -> p b t i", t=PACK, i=4),
-                in_=src.rearrange("p (b i t) -> p b t i", t=PACK, i=4),
-            )
-
-        def deal_small(engine_copy, dst, src):
-            engine_copy(
-                out=dst.rearrange("p (t m) -> p t m", t=PACK),
-                in_=src.rearrange("p (m t) -> p t m", t=PACK),
-            )
-
-        deal_words32(nc.vector.tensor_copy, ka_w[:], ka_raw[:])
-        deal_words32(nc.scalar.copy, kb_w[:], kb_raw[:])
-        deal_small(nc.vector.tensor_copy, ka_s[:], planes1[:, 0:W])
-        deal_small(nc.vector.tensor_copy, kb_s[:], planes1[:, 2 * W:3 * W])
-        deal_words32(nc.scalar.copy, wy_w[:], wy_raw[:])
-        deal_small(nc.scalar.copy, vo_w[:].bitcast(U16), vo_raw[:].bitcast(U16))
-        deal_small(nc.vector.tensor_copy, wy_s[:], planes1[:, 4 * W:5 * W])
-        deal_small(nc.vector.tensor_copy, vo_s[:], planes1[:, 5 * W:6 * W])
-        qa_s = planes1[:, W:2 * W]
-        qb_s = planes1[:, 3 * W:4 * W]
-
-        a_bank = [ps.tile([P, PACK, CH], F32, name="a%d" % c) for c in range(NCH)]
-        y_bank = [ps.tile([P, PACK, CH], F32, name="y%d" % c) for c in range(NCH)]
-        pw_bf = [tile("pw_bf%d" % c, [P, CH * PACK], BF16) for c in range(NCH)]
-        pw_w = [tile("pw_w%d" % c, [P, CH], U32) for c in range(NCH)]
-        pw_s = [tile("pw_s%d" % c, [P, CH], U8) for c in range(NCH)]
-        y_f = [tile("y_f%d" % c, [P, PACK, CH], F32) for c in range(NCH)]
-        y_bf = [tile("y_bf%d" % c, [P, CH * PACK], BF16) for c in range(NCH)]
-        out_rows = out_0.rearrange("(p r) q -> p r q", r=PACK)
-        out_words = words8(out_1)
-
-        def cols(j, width=1):
-            return slice(j * CH * width, (j + 1) * CH * width)
-
-        def fp8_by_fp4(bank, c, w8, s8, w4, s4, first, last):
-            for t in range(PACK):
-                nc.tensor.matmul_mx(
-                    out=bank[:, t, :],
-                    lhsT=w8[:, cols(t)].bitcast(FP8X4), lhsT_scale=s8[:, cols(t)],
-                    rhs=w4[:, cols(c, 2)].bitcast(FP4X4), rhs_scale=s4[:, cols(c)],
-                    start=(first and t == 0), stop=(last and t == PACK - 1),
+        def place_rows(planes, rows, low_queue, high_queue):
+            for quad in (0, 2, 1, 3):
+                (low_queue, high_queue)[quad // 2].dma_start(
+                    out=planes[32 * quad:32 * quad + 4, :].bitcast(I32),
+                    in_=rows[4 * quad:4 * quad + 4, :].bitcast(I32),
                 )
 
-        def scores(c):
+        def deal_words(copy, dst, src):
+            copy(
+                out=dst.rearrange("p (t b i) -> p b t i", t=SLOTS, i=RUN),
+                in_=src.rearrange("p (b i t) -> p b t i", t=SLOTS, i=RUN),
+            )
+
+        def deal_narrow(copy, dst, src, lo=0, hi=SLOTS):
+            copy(
+                out=dst.rearrange("p (t m) -> p t m", t=SLOTS)[:, lo:hi, :],
+                in_=src.rearrange("p (m t) -> p t m", t=SLOTS)[:, lo:hi, :],
+            )
+
+        def fp8_by_fp4(bank, c, w8, s8, w4, s4, opens, closes):
+            for t in range(SLOTS):
+                nc.tensor.matmul_mx(
+                    out=bank[:, t, :],
+                    lhsT=w8[:, cols(t, P)].bitcast(FP8X4), lhsT_scale=s8[:, cols(t, P)],
+                    rhs=w4[:, cols(c, 2 * CH)].bitcast(FP4X4), rhs_scale=s4[:, cols(c, CH)],
+                    start=(opens and t == 0), stop=(closes and t == SLOTS - 1),
+                )
+
+        def scores_first(c):
             fp8_by_fp4(a_bank[c], c, ka_w, ka_s, qa_w, qa_s, True, False)
+
+        def scores_second(c):
             fp8_by_fp4(a_bank[c], c, kb_w, kb_s, qb_w, qb_s, False, True)
 
-        def skip(c):
-            fp8_by_fp4(y_bank[c], c, wy_w, wy_s, qa_w, qa_s, True, False)
+        def scores(c):
+            scores_first(c)
+            scores_second(c)
 
-        def carry(c):
-            for r in range(PACK):
+        def outputs(c):
+            fp8_by_fp4(y_bank[c], c, wy_w, wy_s, qa_w, qa_s, True, False)
+            for t in range(SLOTS):
                 nc.tensor.matmul_mx(
-                    out=y_bank[c][:, r, :],
-                    lhsT=vo_w[:, cols(r, 2)].bitcast(FP4X4), lhsT_scale=vo_s[:, cols(r)],
+                    out=y_bank[c][:, t, :],
+                    lhsT=vo_w[:, cols(t, 2 * P)].bitcast(FP4X4), lhsT_scale=vo_s[:, cols(t, P)],
                     rhs=pw_w[c][:].bitcast(FP8X4), rhs_scale=pw_s[c][:],
-                    start=False, stop=(r == PACK - 1),
+                    start=False, stop=(t == SLOTS - 1),
                 )
 
         def weigh(c):
             nc.vector.scalar_tensor_tensor(
-                out=pw_bf[c][:].rearrange("p (q t) -> p q t", t=PACK),
+                out=pw_bf[c][:].rearrange("p (q t) -> p q t", t=SLOTS),
                 in0=a_bank[c][:].rearrange("p t q -> p q t"),
                 scalar=0.0,
-                in1=fi_t[:].unsqueeze(1).to_broadcast([P, CH, PACK]),
+                in1=fi_t[:].unsqueeze(1).to_broadcast([P, CH, SLOTS]),
                 op0=ALU.max, op1=ALU.mult,
             )
 
         def quantise_pw(c):
             nc.vector.quantize_mx(out=pw_w[c][:].bitcast(FP8X4), scales=pw_s[c][:], in_=pw_bf[c][:])
 
-        def y_out(c):
+        def store_y(c, queue):
             nc.scalar.copy(out=y_f[c][:], in_=y_bank[c][:])
-            nc.sync.dma_start(out=out_rows[:, :, cols(c)], in_=y_f[c][:])
+            queue.dma_start(out=out_0.rearrange("(p t) q -> p t q", t=SLOTS)[:, :, cols(c, CH)], in_=y_f[c][:])
 
-        def y_round_scalar(c):
+        def round_y_from_psum(c):
             nc.scalar.copy(
-                out=y_bf[c][:].rearrange("p (q r) -> p q r", r=PACK),
-                in_=y_bank[c][:].rearrange("p r q -> p q r"),
+                out=y_bf[c][:].rearrange("p (q t) -> p q t", t=SLOTS),
+                in_=y_bank[c][:].rearrange("p t q -> p q t"),
             )
 
-        def y_round_vector(c):
+        def round_y_from_sbuf(c):
             nc.vector.tensor_copy(
-                out=y_bf[c][:].rearrange("p (b i r) -> p b r i", r=PACK, i=4),
-                in_=y_f[c][:].rearrange("p r (b i) -> p b r i", i=4),
+                out=y_bf[c][:].rearrange("p (b i t) -> p b t i", t=SLOTS, i=RUN),
+                in_=y_f[c][:].rearrange("p t (b i) -> p b t i", i=RUN),
             )
 
         def quantise_y(c):
-            nc.vector.quantize_mx(out=y_codes[:, cols(c)].bitcast(FP8X4), scales=y_scales[:, cols(c)], in_=y_bf[c][:])
-            nc.sync.dma_start(out=out_words[:, cols(c)], in_=y_codes[:, cols(c)].bitcast(I32))
+            nc.vector.quantize_mx(
+                out=y_codes[:, cols(c, CH)].bitcast(FP8X4), scales=y_scales[:, cols(c, CH)], in_=y_bf[c][:]
+            )
 
-        scores(0)
+        def store_codes(first, end):
+            span = slice(first * CH, end * CH)
+            nc.sync.dma_start(out=as_words(out_1)[:, span], in_=y_codes[:, span].bitcast(I32))
+
+        nc.vector.memset(score_planes[:].bitcast(U32), 0)
+        nc.vector.memset(out_planes[:].bitcast(U32), 0)
+        nc.gpsimd.dma_start(out=fi_t[:], in_=fi.rearrange("(p t) o -> p (t o)", t=SLOTS))
+        load_rows(score_rows, score_scales)
+        load_rows(out_rows, out_scales)
+        nc.sync.dma_start(out=ka_raw[:].bitcast(I32), in_=as_words(ka_words))
+        nc.scalar.dma_start(out=qa_w[:].bitcast(I32), in_=qa_words[0].bitcast(I32))
+        place_rows(score_planes, score_rows, nc.sync, nc.scalar)
+        nc.sync.dma_start(out=kb_raw[:].bitcast(I32), in_=as_words(kb_words))
+        nc.scalar.dma_start(out=qb_w[:].bitcast(I32), in_=qb_words[0].bitcast(I32))
+        nc.sync.dma_start(out=wy_raw[:].bitcast(I32), in_=as_words(wy_words))
+        nc.sync.dma_start(out=vo_raw[:].bitcast(I32), in_=vo_words[0].bitcast(I32))
+        place_rows(out_planes, out_rows, nc.sync, nc.sync)
+
+        deal_words(nc.vector.tensor_copy, ka_w[:], ka_raw[:])
+        for lo in (0, SLOTS // 2):
+            deal_narrow(nc.vector.tensor_copy, ka_s[:], ka_plane, lo, lo + SLOTS // 2)
+        deal_narrow(nc.vector.tensor_copy, kb_s[:], kb_plane)
+        deal_words(nc.vector.tensor_copy, kb_w[:], kb_raw[:])
+        deal_words(nc.scalar.copy, wy_w[:], wy_raw[:])
+        deal_narrow(nc.scalar.copy, vo_w[:].bitcast(U16), vo_raw[:].bitcast(U16))
+
+        for c in (0, 1):
+            scores_first(c)
+        for c in (0, 1):
+            scores_second(c)
+        deal_narrow(nc.vector.tensor_copy, wy_s[:], wy_plane)
         weigh(0)
+        deal_narrow(nc.vector.tensor_copy, vo_s[:], vo_plane)
         quantise_pw(0)
-        scores(1)
         weigh(1)
-        quantise_pw(1)
-        skip(0)
-        carry(0)
-        y_out(0)
-        y_round_scalar(0)
         scores(2)
         weigh(2)
+        quantise_pw(1)
         quantise_pw(2)
-        skip(1)
-        carry(1)
-        y_out(1)
-        y_round_scalar(1)
+
+        last = CHUNKS - 1
+        outputs(0)
+        store_y(0, nc.sync)
+        round_y_from_psum(0)
+        scores(last)
+        weigh(last)
         quantise_y(0)
-        scores(3)
-        weigh(3)
-        quantise_pw(3)
-        skip(2)
-        carry(2)
-        y_out(2)
-        quantise_y(1)
-        skip(3)
-        carry(3)
-        y_round_vector(2)
-        y_out(3)
-        quantise_y(2)
-        y_round_vector(3)
-        quantise_y(3)
-        for q in range(4):
-            queues[q % 2].dma_start(
-                out=out_2[0, 4 * q:4 * q + 4, :].bitcast(I32), in_=y_scales[32 * q:32 * q + 4, :].bitcast(I32)
+        store_codes(0, 1)
+        quantise_pw(last)
+
+        for c in range(1, last):
+            outputs(c)
+            store_y(c, nc.sync)
+            round_y_from_sbuf(c)
+            if c > 1:
+                quantise_y(c - 1)
+
+        outputs(last)
+        round_y_from_psum(last)
+        quantise_y(last - 1)
+        quantise_y(last)
+        store_y(last, nc.scalar)
+        store_codes(1, CHUNKS)
+        for quad in range(QUADS):
+            queues[(quad + 1) % 2].dma_start(
+                out=out_2[0, 4 * quad:4 * quad + 4, :].bitcast(I32),
+                in_=y_scales[32 * quad:32 * quad + 4, :].bitcast(I32),
             )

@@ -77,9 +77,9 @@ def tile_mix_positive_scores_carry_rows_pl_kernel(
         def as_words(ap):
             return ap[0].rearrange("p c t -> p (c t)").bitcast(I32)
 
-        def load_rows(rows, sources):
+        def load_rows(rows, sources, by_turns):
             for j, src in enumerate(sources):
-                queues[j % 2].dma_start(out=rows[0:BLOCKS, cols(j, W)].bitcast(I32), in_=src[0].bitcast(I32))
+                by_turns[j % len(by_turns)].dma_start(out=rows[0:BLOCKS, cols(j, W)].bitcast(I32), in_=src[0].bitcast(I32))
 
         def place_rows(planes, rows, low_queue, high_queue):
             for quad in (0, 2, 1, 3):
@@ -109,15 +109,9 @@ def tile_mix_positive_scores_carry_rows_pl_kernel(
                     start=(opens and t == 0), stop=(closes and t == SLOTS - 1),
                 )
 
-        def scores_first(c):
-            fp8_by_fp4(a_bank[c], c, ka_w, ka_s, qa_w, qa_s, True, False)
-
-        def scores_second(c):
-            fp8_by_fp4(a_bank[c], c, kb_w, kb_s, qb_w, qb_s, False, True)
-
         def scores(c):
-            scores_first(c)
-            scores_second(c)
+            fp8_by_fp4(a_bank[c], c, ka_w, ka_s, qa_w, qa_s, True, False)
+            fp8_by_fp4(a_bank[c], c, kb_w, kb_s, qb_w, qb_s, False, True)
 
         def outputs(c):
             fp8_by_fp4(y_bank[c], c, wy_w, wy_s, qa_w, qa_s, True, False)
@@ -168,14 +162,14 @@ def tile_mix_positive_scores_carry_rows_pl_kernel(
 
         nc.vector.memset(score_planes[:].bitcast(U32), 0)
         nc.vector.memset(out_planes[:].bitcast(U32), 0)
+        load_rows(out_rows, out_scales, (nc.gpsimd,))
         nc.gpsimd.dma_start(out=fi_t[:], in_=fi.rearrange("(p t) o -> p (t o)", t=SLOTS))
-        load_rows(score_rows, score_scales)
-        load_rows(out_rows, out_scales)
-        nc.sync.dma_start(out=ka_raw[:].bitcast(I32), in_=as_words(ka_words))
-        nc.scalar.dma_start(out=qa_w[:].bitcast(I32), in_=qa_words[0].bitcast(I32))
+        load_rows(score_rows, score_scales, queues)
+        nc.sync.dma_start(out=qa_w[:].bitcast(I32), in_=qa_words[0].bitcast(I32))
+        nc.scalar.dma_start(out=ka_raw[:].bitcast(I32), in_=as_words(ka_words))
+        nc.sync.dma_start(out=qb_w[:].bitcast(I32), in_=qb_words[0].bitcast(I32))
+        nc.scalar.dma_start(out=kb_raw[:].bitcast(I32), in_=as_words(kb_words))
         place_rows(score_planes, score_rows, nc.sync, nc.scalar)
-        nc.sync.dma_start(out=kb_raw[:].bitcast(I32), in_=as_words(kb_words))
-        nc.scalar.dma_start(out=qb_w[:].bitcast(I32), in_=qb_words[0].bitcast(I32))
         nc.sync.dma_start(out=wy_raw[:].bitcast(I32), in_=as_words(wy_words))
         nc.sync.dma_start(out=vo_raw[:].bitcast(I32), in_=vo_words[0].bitcast(I32))
         place_rows(out_planes, out_rows, nc.sync, nc.sync)
@@ -184,18 +178,16 @@ def tile_mix_positive_scores_carry_rows_pl_kernel(
         for lo in (0, SLOTS // 2):
             deal_narrow(nc.vector.tensor_copy, ka_s[:], ka_plane, lo, lo + SLOTS // 2)
         deal_narrow(nc.vector.tensor_copy, kb_s[:], kb_plane)
-        deal_words(nc.vector.tensor_copy, kb_w[:], kb_raw[:])
+        deal_words(nc.scalar.copy, kb_w[:], kb_raw[:])
         deal_words(nc.scalar.copy, wy_w[:], wy_raw[:])
         deal_narrow(nc.scalar.copy, vo_w[:].bitcast(U16), vo_raw[:].bitcast(U16))
 
-        for c in (0, 1):
-            scores_first(c)
-        for c in (0, 1):
-            scores_second(c)
-        deal_narrow(nc.vector.tensor_copy, wy_s[:], wy_plane)
+        scores(0)
         weigh(0)
+        deal_narrow(nc.vector.tensor_copy, wy_s[:], wy_plane)
         deal_narrow(nc.vector.tensor_copy, vo_s[:], vo_plane)
         quantise_pw(0)
+        scores(1)
         weigh(1)
         scores(2)
         weigh(2)

from contextlib import ExitStack

import concourse.mybir as mybir

F32 = mybir.dt.float32
BF16 = mybir.dt.bfloat16
I32 = mybir.dt.int32
U32 = mybir.dt.uint32
U16 = mybir.dt.uint16
U8 = mybir.dt.uint8
FP8X4 = mybir.dt.float8_e4m3fn_x4
FP4X4 = mybir.dt.float4_e2m1fn_x4
ALU = mybir.AluOpType

P = 128
SLOTS = 4
W = 512
CH = 128
CHUNKS = W // CH
BLOCKS = 16
QUADS = 4
RUN = 4
FLOPS = 4 * 2 * W * W * W


def tile_mix_positive_scores_carry_rows_pl_kernel(
    tc, qa_words, qa_scales, ka_words, ka_scales, qb_words, qb_scales, kb_words, kb_scales,
    fi, vo_words, vo_scales, wy_words, wy_scales, out_0, out_1, out_2,
):
    nc = tc.nc
    queues = (nc.sync, nc.scalar)
    with ExitStack() as ctx:
        sb = ctx.enter_context(tc.tile_pool(name="sb", bufs=1))
        ps = ctx.enter_context(tc.psum_pool(name="ps", bufs=1))
        ctx.enter_context(tc.manual_schedule())

        def tile(name, shape, dtype):
            return sb.tile(shape, dtype, name=name, align_bytes=64)

        def cols(j, width):
            return slice(j * width, (j + 1) * width)

        ka_raw = tile("ka_raw", [P, W], U32)
        kb_raw = tile("kb_raw", [P, W], U32)
        wy_raw = tile("wy_raw", [P, W], U32)
        vo_raw = tile("vo_raw", [P, 2 * W], U8)
        qa_w = tile("qa_w", [P, 2 * W], U8)
        qb_w = tile("qb_w", [P, 2 * W], U8)
        ka_w = tile("ka_w", [P, W], U32)
        kb_w = tile("kb_w", [P, W], U32)
        wy_w = tile("wy_w", [P, W], U32)
        vo_w = tile("vo_w", [P, 2 * W], U8)
        ka_s = tile("ka_s", [P, W], U8)
        kb_s = tile("kb_s", [P, W], U8)
        wy_s = tile("wy_s", [P, W], U8)
        vo_s = tile("vo_s", [P, W], U8)
        score_scales = (ka_scales, qa_scales, kb_scales, qb_scales)
        out_scales = (wy_scales, vo_scales)
        score_rows = tile("score_rows", [BLOCKS, len(score_scales) * W], U8)
        score_planes = tile("score_planes", [P, len(score_scales) * W], U8)
        out_rows = tile("out_rows", [BLOCKS, len(out_scales) * W], U8)
        out_planes = tile("out_planes", [P, len(out_scales) * W], U8)
        ka_plane, qa_s, kb_plane, qb_s = [score_planes[:, cols(j, W)] for j in range(len(score_scales))]
        wy_plane, vo_plane = [out_planes[:, cols(j, W)] for j in range(len(out_scales))]
        fi_t = tile("fi_t", [P, SLOTS], F32)
        y_codes = tile("y_codes", [P, W], U32)
        y_scales = tile("y_scales", [P, W], U8)

        a_bank = [ps.tile([P, SLOTS, CH], F32, name="a%d" % c) for c in range(CHUNKS)]
        y_bank = [ps.tile([P, SLOTS, CH], F32, name="y%d" % c) for c in range(CHUNKS)]
        pw_bf = [tile("pw_bf%d" % c, [P, CH * SLOTS], BF16) for c in range(CHUNKS)]
        pw_w = [tile("pw_w%d" % c, [P, CH], U32) for c in range(CHUNKS)]
        pw_s = [tile("pw_s%d" % c, [P, CH], U8) for c in range(CHUNKS)]
        y_f = [tile("y_f%d" % c, [P, SLOTS, CH], F32) for c in range(CHUNKS)]
        y_bf = [tile("y_bf%d" % c, [P, CH * SLOTS], BF16) for c in range(CHUNKS)]

        def as_words(ap):
            return ap[0].rearrange("p c t -> p (c t)").bitcast(I32)

        def load_rows(rows, sources, by_turns):
            for j, src in enumerate(sources):
                by_turns[j % len(by_turns)].dma_start(out=rows[0:BLOCKS, cols(j, W)].bitcast(I32), in_=src[0].bitcast(I32))

        def place_rows(planes, rows, low_queue, high_queue):
            for quad in (0, 2, 1, 3):
                (low_queue, high_queue)[quad // 2].dma_start(
                    out=planes[32 * quad:32 * quad + 4, :].bitcast(I32),
                    in_=rows[4 * quad:4 * quad + 4, :].bitcast(I32),
                )

        def deal_words(copy, dst, src):
            copy(
                out=dst.rearrange("p (t b i) -> p b t i", t=SLOTS, i=RUN),
                in_=src.rearrange("p (b i t) -> p b t i", t=SLOTS, i=RUN),
            )

        def deal_narrow(copy, dst, src, lo=0, hi=SLOTS):
            copy(
                out=dst.rearrange("p (t m) -> p t m", t=SLOTS)[:, lo:hi, :],
                in_=src.rearrange("p (m t) -> p t m", t=SLOTS)[:, lo:hi, :],
            )

        def fp8_by_fp4(bank, c, w8, s8, w4, s4, opens, closes):
            for t in range(SLOTS):
                nc.tensor.matmul_mx(
                    out=bank[:, t, :],
                    lhsT=w8[:, cols(t, P)].bitcast(FP8X4), lhsT_scale=s8[:, cols(t, P)],
                    rhs=w4[:, cols(c, 2 * CH)].bitcast(FP4X4), rhs_scale=s4[:, cols(c, CH)],
                    start=(opens and t == 0), stop=(closes and t == SLOTS - 1),
                )

        def scores(c):
            fp8_by_fp4(a_bank[c], c, ka_w, ka_s, qa_w, qa_s, True, False)
            fp8_by_fp4(a_bank[c], c, kb_w, kb_s, qb_w, qb_s, False, True)

        def outputs(c):
            fp8_by_fp4(y_bank[c], c, wy_w, wy_s, qa_w, qa_s, True, False)
            for t in range(SLOTS):
                nc.tensor.matmul_mx(
                    out=y_bank[c][:, t, :],
                    lhsT=vo_w[:, cols(t, 2 * P)].bitcast(FP4X4), lhsT_scale=vo_s[:, cols(t, P)],
                    rhs=pw_w[c][:].bitcast(FP8X4), rhs_scale=pw_s[c][:],
                    start=False, stop=(t == SLOTS - 1),
                )

        def weigh(c):
            nc.vector.scalar_tensor_tensor(
                out=pw_bf[c][:].rearrange("p (q t) -> p q t", t=SLOTS),
                in0=a_bank[c][:].rearrange("p t q -> p q t"),
                scalar=0.0,
                in1=fi_t[:].unsqueeze(1).to_broadcast([P, CH, SLOTS]),
                op0=ALU.max, op1=ALU.mult,
            )

        def quantise_pw(c):
            nc.vector.quantize_mx(out=pw_w[c][:].bitcast(FP8X4), scales=pw_s[c][:], in_=pw_bf[c][:])

        def store_y(c, queue):
            nc.scalar.copy(out=y_f[c][:], in_=y_bank[c][:])
            queue.dma_start(out=out_0.rearrange("(p t) q -> p t q", t=SLOTS)[:, :, cols(c, CH)], in_=y_f[c][:])

        def round_y_from_psum(c):
            nc.scalar.copy(
                out=y_bf[c][:].rearrange("p (q t) -> p q t", t=SLOTS),
                in_=y_bank[c][:].rearrange("p t q -> p q t"),
            )

        def round_y_from_sbuf(c):
            nc.vector.tensor_copy(
                out=y_bf[c][:].rearrange("p (b i t) -> p b t i", t=SLOTS, i=RUN),
                in_=y_f[c][:].rearrange("p t (b i) -> p b t i", i=RUN),
            )

        def quantise_y(c):
            nc.vector.quantize_mx(
                out=y_codes[:, cols(c, CH)].bitcast(FP8X4), scales=y_scales[:, cols(c, CH)], in_=y_bf[c][:]
            )

        def store_codes(first, end):
            span = slice(first * CH, end * CH)
            nc.sync.dma_start(out=as_words(out_1)[:, span], in_=y_codes[:, span].bitcast(I32))

        nc.vector.memset(score_planes[:].bitcast(U32), 0)
        nc.vector.memset(out_planes[:].bitcast(U32), 0)
        load_rows(out_rows, out_scales, (nc.gpsimd,))
        nc.gpsimd.dma_start(out=fi_t[:], in_=fi.rearrange("(p t) o -> p (t o)", t=SLOTS))
        load_rows(score_rows, score_scales, queues)
        nc.sync.dma_start(out=qa_w[:].bitcast(I32), in_=qa_words[0].bitcast(I32))
        nc.scalar.dma_start(out=ka_raw[:].bitcast(I32), in_=as_words(ka_words))
        nc.sync.dma_start(out=qb_w[:].bitcast(I32), in_=qb_words[0].bitcast(I32))
        nc.scalar.dma_start(out=kb_raw[:].bitcast(I32), in_=as_words(kb_words))
        place_rows(score_planes, score_rows, nc.sync, nc.scalar)
        nc.sync.dma_start(out=wy_raw[:].bitcast(I32), in_=as_words(wy_words))
        nc.sync.dma_start(out=vo_raw[:].bitcast(I32), in_=vo_words[0].bitcast(I32))
        place_rows(out_planes, out_rows, nc.sync, nc.sync)

        deal_words(nc.vector.tensor_copy, ka_w[:], ka_raw[:])
        for lo in (0, SLOTS // 2):
            deal_narrow(nc.vector.tensor_copy, ka_s[:], ka_plane, lo, lo + SLOTS // 2)
        deal_narrow(nc.vector.tensor_copy, kb_s[:], kb_plane)
        deal_words(nc.scalar.copy, kb_w[:], kb_raw[:])
        deal_words(nc.scalar.copy, wy_w[:], wy_raw[:])
        deal_narrow(nc.scalar.copy, vo_w[:].bitcast(U16), vo_raw[:].bitcast(U16))

        scores(0)
        weigh(0)
        deal_narrow(nc.vector.tensor_copy, wy_s[:], wy_plane)
        deal_narrow(nc.vector.tensor_copy, vo_s[:], vo_plane)
        quantise_pw(0)
        scores(1)
        weigh(1)
        scores(2)
        weigh(2)
        quantise_pw(1)
        quantise_pw(2)

        last = CHUNKS - 1
        outputs(0)
        store_y(0, nc.sync)
        round_y_from_psum(0)
        scores(last)
        weigh(last)
        quantise_y(0)
        store_codes(0, 1)
        quantise_pw(last)

        for c in range(1, last):
            outputs(c)
            store_y(c, nc.sync)
            round_y_from_sbuf(c)
            if c > 1:
                quantise_y(c - 1)

        outputs(last)
        round_y_from_psum(last)
        quantise_y(last - 1)
        quantise_y(last)
        store_y(last, nc.scalar)
        store_codes(1, CHUNKS)
        for quad in range(QUADS):
            queues[(quad + 1) % 2].dma_start(
                out=out_2[0, 4 * quad:4 * quad + 4, :].bitcast(I32),
                in_=y_scales[32 * quad:32 * quad + 4, :].bitcast(I32),
            )
